import numpy as np
import ml_dtypes


def mxq(x, axis, fmt="e4m3"):
    dtype, down = {"e4m3": (ml_dtypes.float8_e4m3fn, 7), "e5m2": (ml_dtypes.float8_e5m2, 14)}[fmt]
    v = np.moveaxis(np.asarray(x, np.float32).astype(ml_dtypes.bfloat16).astype(np.float64), axis, -1)
    blocks = v.reshape(v.shape[:-1] + (-1, 32))
    amax = np.abs(blocks).max(-1, keepdims=True)
    byte = np.maximum(np.where(amax > 0, np.frexp(amax)[1] - 1 + 127, 0) - down, 1)
    scale = np.exp2(byte - 127.0)
    codes = (blocks / scale).astype(np.float32).astype(dtype).astype(np.float64)
    return np.moveaxis((codes * scale).reshape(v.shape), -1, axis)


WIDE = False


def mx_kscale(k):
    if not WIDE:
        return np.ones(k)
    levels = np.array([30, -30])
    if k % 512:
        return np.exp2(np.random.permutation(np.resize(levels, k // 32))).repeat(32)
    a = np.empty((k // 512, 16))
    for p in range(k // 512):
        a[p, :8] = np.random.permutation(np.resize(levels, 8))
        for g in range(8):
            far = levels[np.abs(levels - a[p, g]) >= 10]
            a[p, g + 8] = far[np.random.randint(len(far))]
    return np.exp2(a.ravel()).repeat(32)


BF16 = ml_dtypes.bfloat16


def bf(x):
    return np.asarray(x, np.float32).astype(BF16)


def f64(x):
    return np.asarray(x).astype(np.float64)


E2M1 = np.array([0.0, 0.5, 1.0, 1.5, 2.0, 3.0, 4.0, 6.0, -0.0, -0.5, -1.0, -1.5, -2.0, -3.0, -4.0, -6.0])


def pack_weight(w, fmt):
    k, n = w.shape
    w = f64(bf(w)).reshape(k // 32, 32, n)
    amax = np.abs(w).max(1)
    if fmt == "e4m3":
        byte = np.frexp(amax)[1] - 1 + 127 - 7
    else:
        mant, ex = np.frexp(amax / 6.0)
        byte = np.where(mant > 0.5, ex, ex - 1) + 127
    byte = np.clip(np.where(amax > 0, byte, 1), 1, 254)
    scaled = (w * np.exp2(127.0 - byte)[:, None, :]).reshape(k, n).astype(np.float32)
    by_word = np.ascontiguousarray(scaled.reshape(k // 512, 128, 4, n).transpose(0, 1, 3, 2))
    if fmt == "e4m3":
        words = by_word.astype(ml_dtypes.float8_e4m3fn).view(np.uint8)
    else:
        c = by_word.astype(ml_dtypes.float4_e2m1fn).view(np.uint8) & 0xF
        words = c[..., 0::2] | (c[..., 1::2] << 4)
    return np.ascontiguousarray(words), np.ascontiguousarray(byte.astype(np.uint8).reshape(k // 512, 16, n))


def unpack_weight(words, scales, fmt):
    g, p, n, _ = words.shape
    if fmt == "e4m3":
        vals = np.ascontiguousarray(words).view(ml_dtypes.float8_e4m3fn).astype(np.float64)
    else:
        nib = np.empty((g, p, n, 4), np.uint8)
        nib[..., 0::2] = words & 0xF
        nib[..., 1::2] = words >> 4
        vals = E2M1[nib]
    vals = vals * np.repeat(np.exp2(scales.astype(np.float64) - 127.0), 8, axis=1)[..., None]
    return vals.transpose(0, 1, 3, 2).reshape(g * 512, n)
def pack4(w):
    words, scales = pack_weight(w, "e2m1")
    return words.reshape(words.shape[0], 128, -1), scales


def unpack4(words, scales):
    return unpack_weight(words.reshape(words.shape[0], 128, -1, 2), scales, "e2m1")


M, N, Q, KI, KT, D = 1024, 1024, 1024, 1536, 1024, 1024


def setup_inputs():
    s, r, t = mx_kscale(KI), mx_kscale(KT), mx_kscale(D)
    wi_words, wi_scales = pack4(np.random.standard_normal((KI, D)) / np.sqrt(KI) / s[:, None])
    wt_words, wt_scales = pack4(np.random.standard_normal((KT, D)) / np.sqrt(KT) / r[:, None] / t)
    return {"img": bf(np.random.standard_normal((M, KI)) * s),
            "wi_words": wi_words, "wi_scales": wi_scales,
            "bi": bf(0.3 * np.random.standard_normal(D)),
            "gain": bf((1 + 0.1 * np.random.standard_normal(D)) * t),
            "txt": bf(np.random.standard_normal((N, KT)) * r),
            "wt_words": wt_words, "wt_scales": wt_scales,
            "bt": bf(0.3 * np.random.standard_normal(D) / t),
            "queue": bf(np.random.standard_normal((Q, D)) / t),
            "tau": bf((1 + 0.1 * np.random.standard_normal(M)) * 2 / np.sqrt(D))}


def reference(img, wi_words, wi_scales, bi, gain, txt, wt_words, wt_scales, bt, queue, tau):
    u = ((mxq(f64(img), 1, "e4m3") @ unpack4(wi_words, wi_scales)) + f64(bi)) * f64(gain)
    v = (mxq(f64(txt), 1, "e4m3") @ unpack4(wt_words, wt_scales)) + f64(bt)
    uq = mxq(u, 1, "e5m2")
    batch = (uq @ mxq(v, 1, "e4m3").T) * f64(tau)[:, None]
    stored = (uq @ mxq(f64(queue), 1, "e4m3").T) * f64(tau)[:, None]
    return batch, stored

@@ -1,0 +1,345 @@
+from contextlib import ExitStack
+
+import concourse.mybir as mybir
+from concourse.masks import make_identity
+
+M, N, Q, KI, KT, D = 1024, 1024, 1024, 1536, 1024, 1024
+FLOPS = 2 * M * KI * D + 2 * N * KT * D + 2 * M * D * (N + Q)
+
+F32 = mybir.dt.float32
+BF16 = mybir.dt.bfloat16
+I32 = mybir.dt.int32
+U32 = mybir.dt.uint32
+U8 = mybir.dt.uint8
+E4M3 = mybir.dt.float8_e4m3fn_x4
+E5M2 = mybir.dt.float8_e5m2_x4
+E2M1 = mybir.dt.float4_e2m1fn_x4
+IDENT = mybir.ActivationFunctionType.Identity
+ADD = mybir.AluOpType.add
+MULT = mybir.AluOpType.mult
+
+P = 128
+KP = 512
+CH = 512
+PAIR = 256
+
+
+def tile_two_tower_queue_logits_s9_kernel(
+    tc, img, wi_words, wi_scales, bi, gain, txt, wt_words, wt_scales, bt, queue, tau, out_0, out_1
+):
+    nc = tc.nc
+    with ExitStack() as ctx:
+        keep = ctx.enter_context(tc.tile_pool(name="keep", bufs=1))
+        stage = ctx.enter_context(tc.tile_pool(name="stage", bufs=1))
+        psum = ctx.enter_context(tc.psum_pool(name="psum", bufs=8))
+        ctx.enter_context(tc.manual_schedule())
+
+        source = {"img": img, "txt": txt, "queue": queue}
+        passes = {"img": KI // KP, "txt": KT // KP, "queue": D // KP}
+        words_in = {"img": wi_words, "txt": wt_words}
+        scales_in = {"img": wi_scales, "txt": wt_scales}
+        raw, ordered, turned = {}, {}, {}
+        w_raw, s_raw, w_codes, w_scales = {}, {}, {}, {}
+        codes, scales, planar, woven, results = {}, {}, {}, {}, {}
+
+        def new_bank():
+            return psum.tile([P, CH], F32, name="bank", tag="bank")
+
+        def mx_tiles(key):
+            if key not in codes:
+                label = "_".join(str(k) for k in key)
+                codes[key] = keep.tile([P, CH], U32, name="codes_" + label, align_bytes=64)
+                scales[key] = keep.tile([P, CH], U8, name="scales_" + label, align_bytes=64)
+            return codes[key], scales[key]
+
+        def load_rows(x, pair):
+            k = source[x].shape[1]
+            raw[x, pair] = keep.tile([P, 2, k], BF16, name="raw_%s_%d" % (x, pair), align_bytes=64)
+            rows = source[x][pair * PAIR : (pair + 1) * PAIR, :]
+            nc.sync.dma_start(out=raw[x, pair][:], in_=rows.rearrange("(p j) k -> p j k", j=2))
+
+        def clear_scale_rows(x, engine):
+            s_raw[x] = keep.tile([P, passes[x], D // 4], I32, name="s_raw_" + x, align_bytes=64)
+            engine.memset(s_raw[x][:], 0)
+
+        def load_words(x, h):
+            w_raw[x, h] = keep.tile([P, passes[x], KP // 2], I32, name="w_raw_%s_%d" % (x, h), align_bytes=64)
+            half = words_in[x].bitcast(I32)[:, :, h * KP // 2 : (h + 1) * KP // 2]
+            nc.sync.dma_start(out=w_raw[x, h][:], in_=half.rearrange("g p n -> p g n"))
+
+        def load_scale_rows(x, engine):
+            rows = scales_in[x].bitcast(I32)
+            for quad in range(4):
+                engine.dma_start(
+                    out=s_raw[x][32 * quad : 32 * quad + 4, :, :],
+                    in_=rows[:, 4 * quad : 4 * quad + 4, :].rearrange("g r n -> r g n"),
+                )
+
+        def order_words(x, h):
+            w_codes[x, h] = keep.tile([P, passes[x] * 2 * KP], U8, name="w_codes_%s_%d" % (x, h), align_bytes=256)
+            nc.vector.tensor_copy(
+                out=w_codes[x, h][:].bitcast(I32).rearrange("p (g t q i) -> p g q t i", t=4, q=16, i=4),
+                in_=w_raw[x, h][:].rearrange("p g (q t i) -> p g q t i", t=4, i=4),
+            )
+
+        def order_scales(x):
+            w_scales[x] = keep.tile([P, passes[x] * D], U8, name="w_scales_" + x, align_bytes=256)
+            nc.vector.tensor_copy(
+                out=w_scales[x][:].bitcast(I32).rearrange("p (h t q i) -> p h t q i", t=4, q=16, i=2),
+                in_=s_raw[x][:].rearrange("p g (h q t i) -> p (g h) t q i", q=16, t=4, i=2),
+            )
+
+        def sort(x, pair):
+            k = source[x].shape[1]
+            ordered[x, pair] = stage.tile([P, 2, k // 2], F32, name="ordered", tag="ordered", bufs=3, align_bytes=64)
+            flat = raw[x, pair][:].rearrange("p j k -> p (j k)")
+            if x == "queue":
+                nc.vector.tensor_copy(
+                    out=ordered[x, pair][:].bitcast(BF16).rearrange("p u (b r e) -> p b u r e", r=8, e=2),
+                    in_=flat.rearrange("p (b u e r) -> p b u r e", u=2, e=2, r=8),
+                )
+            else:
+                nc.vector.tensor_copy(
+                    out=ordered[x, pair][:].rearrange("p u (c i) -> p c u i", i=4),
+                    in_=flat.bitcast(F32).rearrange("p (c i u) -> p c u i", i=4, u=2),
+                )
+
+        def turn(x, pair, engines):
+            for g in range(passes[x]):
+                bank = new_bank()
+                quarters = bank[:].rearrange("p (j u r) -> p j u r", j=2, u=2)
+                for j in range(2):
+                    for u in range(2):
+                        first = (j * passes[x] + g) * P
+                        if (x, pair) in ordered:
+                            block = ordered[x, pair][:, u, first : first + P]
+                        else:
+                            flat = raw[x, pair][:].rearrange("p j k -> p (j k)").bitcast(F32)
+                            block = flat[:, 2 * first + u : 2 * (first + P) : 2]
+                        nc.tensor.transpose(quarters[:, j, u, :], block, ident[:])
+                turned[x, pair, g] = stage.tile([P, CH], F32, name="turned", tag="turned", bufs=8, align_bytes=64)
+                out = turned[x, pair, g][:].rearrange("p (r v) -> p r v", v=4)
+                in_ = bank[:].rearrange("p (v r) -> p r v", v=4)
+                if engines[g] == "s":
+                    nc.scalar.copy(out=out, in_=in_)
+                else:
+                    nc.vector.tensor_copy(out=out, in_=in_)
+
+        def quantize_rows(x, pair):
+            half = slice((pair % 2) * PAIR, (pair % 2 + 1) * PAIR)
+            for g in range(passes[x]):
+                c, s = mx_tiles((x, pair // 2, g))
+                nc.vector.quantize_mx(
+                    out=c[:, half].bitcast(E4M3), scales=s[:, half], in_=turned[x, pair, g][:].bitcast(BF16)
+                )
+
+        def tower(x, chunk, h, slots, engines):
+            if (x, chunk, h) not in planar:
+                planar[x, chunk, h] = stage.tile([P, 4, CH], BF16, name="planar", tag="planar", bufs=3, align_bytes=64)
+            for t, engine in zip(slots, engines):
+                bank = new_bank()
+                for g in range(passes[x]):
+                    col = ((2 * g + h) * 4 + t) * P
+                    nc.tensor.matmul_mx(
+                        out=bank[:],
+                        lhsT=w_codes[x, h][:, 2 * (4 * g + t) * P : 2 * (4 * g + t + 1) * P].bitcast(E2M1),
+                        lhsT_scale=w_scales[x][:, col : col + P],
+                        rhs=codes[x, chunk, g][:].bitcast(E4M3),
+                        rhs_scale=scales[x, chunk, g][:],
+                        start=(g == 0),
+                        stop=(g == passes[x] - 1),
+                    )
+                out = planar[x, chunk, h][:, t, :]
+                bi_col = consts[:, 4 * h + t, 0:1]
+                gain_col = consts[:, 4 * h + t, 1:2]
+                bt_col = consts[:, 4 * h + t, 2:3]
+                if x == "img" and engine == "s":
+                    nc.scalar.activation(out=out, in_=bank[:], func=IDENT, bias=bi_gain[:, 4 * h + t, :], scale=gain_col)
+                elif x == "img":
+                    nc.vector.tensor_scalar(out=out, in0=bank[:], scalar1=bi_col, scalar2=gain_col, op0=ADD, op1=MULT)
+                elif engine == "s":
+                    nc.scalar.activation(out=out, in_=bank[:], func=IDENT, bias=bt_col, scale=1.0)
+                else:
+                    nc.vector.tensor_scalar(out=out, in0=bank[:], scalar1=bt_col, scalar2=None, op0=ADD)
+
+        def weave(x, chunk, h):
+            woven[x, chunk, h] = stage.tile([P, CH, 4], BF16, name="woven", tag="woven", bufs=2, align_bytes=64)
+            nc.vector.tensor_copy(
+                out=woven[x, chunk, h][:].rearrange("p (c i) t -> p c t i", i=4),
+                in_=planar[x, chunk, h][:].rearrange("p t (c i) -> p c t i", i=4),
+            )
+
+        def quantize_embedding(x, chunk, h):
+            c, s = mx_tiles(("emb_" + x, chunk, h))
+            nc.vector.quantize_mx(
+                out=c[:].bitcast(E5M2 if x == "img" else E4M3),
+                scales=s[:],
+                in_=woven[x, chunk, h][:].rearrange("p c t -> p (c t)"),
+            )
+
+        def logits(tiles, partner, chunk, engines, joined=2):
+            dest = out_1 if partner == "queue" else out_0
+            for m, engine in zip(tiles, engines):
+                bank = new_bank()
+                cols = slice((m % 4) * P, (m % 4 + 1) * P)
+                for h in range(2):
+                    nc.tensor.matmul_mx(
+                        out=bank[:],
+                        lhsT=codes["emb_img", m // 4, h][:, cols].bitcast(E5M2),
+                        lhsT_scale=scales["emb_img", m // 4, h][:, cols],
+                        rhs=codes[partner, chunk, h][:].bitcast(E4M3),
+                        rhs_scale=scales[partner, chunk, h][:],
+                        start=(h == 0),
+                        stop=(h == 1),
+                    )
+                if m % 2 == 0:
+                    results[partner, chunk, m // 2] = stage.tile([P, 2, CH], F32, name="result", tag="result", bufs=5, align_bytes=64)
+                both = results[partner, chunk, m // 2]
+                result = both[:, m % 2, :]
+                tau_col = consts[:, 0, 32 + m : 33 + m]
+                if engine == "s":
+                    nc.scalar.activation(out=result, in_=bank[:], func=IDENT, bias=0.0, scale=tau_col)
+                else:
+                    nc.vector.tensor_scalar(out=result, in0=bank[:], scalar1=tau_col, scalar2=None, op0=MULT)
+                out_cols = slice(chunk * CH, (chunk + 1) * CH)
+                if joined == 1:
+                    nc.sync.dma_start(out=dest[m * P : (m + 1) * P, out_cols], in_=result)
+                elif m % 2 == 1:
+                    rows = dest[(m - 1) * P : (m + 1) * P, out_cols]
+                    nc.sync.dma_start(out=rows.rearrange("(j p) n -> p j n", j=2), in_=both[:])
+
+        ident = keep.tile([P, P], F32, name="ident", align_bytes=64)
+        vec_rows = keep.tile([3, D], BF16, name="vec_rows", align_bytes=64)
+        tau_rows = keep.tile([40, P], BF16, name="tau_rows", align_bytes=64)
+        vec_wide = keep.tile([P, D], F32, name="vec_wide", align_bytes=64)
+        consts = keep.tile([P, 8, 40], F32, name="consts", align_bytes=64)
+        bi_gain = keep.tile([P, 8, 1], F32, name="bi_gain", align_bytes=64)
+        warm = keep.tile([P, 2], F32, name="warm", align_bytes=64)
+
+        def load_vectors():
+            for v, vec in enumerate((bi, gain, bt)):
+                nc.scalar.dma_start(out=vec_rows[v : v + 1, :], in_=vec.rearrange("(a d) -> a d", a=1))
+            nc.scalar.dma_start(out=tau_rows[32:40, :], in_=tau.rearrange("(m p) -> m p", p=P))
+
+        def widen_vectors():
+            nc.vector.tensor_copy(
+                out=vec_wide[0:3, :].rearrange("v (h t q r) -> v h q t r", h=2, t=4, r=8),
+                in_=vec_rows[:].rearrange("v (h q t r) -> v h q t r", h=2, t=4, r=8),
+            )
+            nc.vector.tensor_copy(out=vec_wide[32:40, 0:P], in_=tau_rows[32:40, :])
+
+        def turn_vectors():
+            for h in range(2):
+                bank = new_bank()
+                for t in range(4):
+                    first = (4 * h + t) * P
+                    nc.tensor.transpose(bank[:, t * P : (t + 1) * P], vec_wide[:, first : first + P], ident[:])
+                nc.scalar.copy(
+                    out=consts[:, 4 * h : 4 * h + 4, :], in_=bank[:].rearrange("p (t c) -> p t c", t=4)[:, :, 0:40]
+                )
+
+        def fold_bias():
+            nc.vector.tensor_tensor(out=bi_gain[:], in0=consts[:, :, 0:1], in1=consts[:, :, 1:2], op=MULT)
+
+        make_identity(nc, ident[:])
+        clear_scale_rows("txt", nc.vector)
+        nc.vector.memset(warm[:, 0:1], 0.0)
+        nc.vector.memset(vec_wide[:], 0.0)
+        clear_scale_rows("img", nc.vector)
+
+        load_vectors()
+        load_rows("txt", 0)
+        load_rows("txt", 1)
+        nc.scalar.activation(out=warm[:, 1:2], in_=warm[:, 0:1], func=IDENT, bias=0.0, scale=1.0)
+        load_scale_rows("txt", nc.gpsimd)
+        load_scale_rows("img", nc.gpsimd)
+        load_words("txt", 0)
+        load_words("txt", 1)
+        load_rows("img", 0)
+        load_rows("img", 1)
+        load_words("img", 0)
+        load_words("img", 1)
+        for x, pair in (("img", 2), ("img", 3), ("queue", 0), ("queue", 1), ("txt", 2), ("txt", 3), ("queue", 2), ("queue", 3)):
+            load_rows(x, pair)
+        A, B = (0, 1), (2, 3)
+        widen_vectors()
+        turn("txt", 0, "ss")
+        quantize_rows("txt", 0)
+        turn("txt", 1, "ss")
+        order_words("txt", 0)
+        order_scales("txt")
+        turn_vectors()
+        quantize_rows("txt", 1)
+        order_words("txt", 1)
+        fold_bias()
+        sort("img", 0)
+        sort("img", 1)
+        tower("txt", 0, 0, A, "ss")
+        turn("img", 0, "svs")
+        tower("txt", 0, 0, B, "ss")
+        quantize_rows("img", 0)
+        turn("img", 1, "svs")
+        order_scales("img")
+        order_words("img", 0)
+        tower("txt", 0, 1, range(4), "ssss")
+        quantize_rows("img", 1)
+        order_words("img", 1)
+        sort("img", 2)
+        tower("img", 0, 0, range(4), "ssss")
+        weave("txt", 0, 0)
+        turn("img", 2, "sss")
+        sort("img", 3)
+        quantize_embedding("txt", 0, 0)
+        weave("txt", 0, 1)
+        tower("img", 0, 1, A, "ss")
+        quantize_rows("img", 2)
+        quantize_embedding("txt", 0, 1)
+        turn("img", 3, "sss")
+        weave("img", 0, 0)
+        tower("img", 0, 1, B, "ss")
+        quantize_rows("img", 3)
+        quantize_embedding("img", 0, 0)
+        sort("queue", 0)
+        weave("img", 0, 1)
+        tower("img", 1, 0, range(4), "ssss")
+        turn("queue", 0, "ss")
+        quantize_embedding("img", 0, 1)
+        sort("queue", 1)
+        quantize_rows("queue", 0)
+        weave("img", 1, 0)
+        tower("img", 1, 1, A, "ss")
+        logits(A, "emb_txt", 0, "ss")
+        turn("queue", 1, "ss")
+        sort("txt", 2)
+        quantize_embedding("img", 1, 0)
+        tower("img", 1, 1, B, "ss")
+        quantize_rows("queue", 1)
+        logits(B, "emb_txt", 0, "sv")
+        turn("txt", 2, "ss")
+        sort("txt", 3)
+        weave("img", 1, 1)
+        logits(A, "queue", 0, "ss")
+        quantize_rows("txt", 2)
+        turn("txt", 3, "ss")
+        quantize_embedding("img", 1, 1)
+        logits(B, "queue", 0, "ss")
+        quantize_rows("txt", 3)
+        sort("queue", 2)
+        logits((4, 5), "emb_txt", 0, "sv")
+        tower("txt", 1, 0, range(4), "svss")
+        turn("queue", 2, "ss")
+        sort("queue", 3)
+        weave("txt", 1, 0)
+        tower("txt", 1, 1, A, "ss")
+        quantize_rows("queue", 2)
+        logits((6, 7), "emb_txt", 0, "ss")
+        quantize_embedding("txt", 1, 0)
+        tower("txt", 1, 1, B, "sv")
+        turn("queue", 3, "ss")
+        weave("txt", 1, 1)
+        logits(range(4, 8), "queue", 0, "ssss")
+        quantize_rows("queue", 3)
+        quantize_embedding("txt", 1, 1)
+        logits(range(0, 8), "queue", 1, "svsvsvsv")
+        logits(range(0, 6), "emb_txt", 1, "svsvsv")
+        logits((6, 7), "emb_txt", 1, "sv", joined=1)

@@ -38,7 +38,7 @@ def tile_two_tower_queue_logits_s9_kernel(
         passes = {"img": KI // KP, "txt": KT // KP, "queue": D // KP}
         words_in = {"img": wi_words, "txt": wt_words}
         scales_in = {"img": wi_scales, "txt": wt_scales}
-        raw, ordered, turned = {}, {}, {}
+        raw, ordered, turned, first_rows = {}, {}, {}, {}
         w_raw, s_raw, w_codes, w_scales = {}, {}, {}, {}
         codes, scales, planar, woven, results = {}, {}, {}, {}, {}
 
@@ -89,9 +89,9 @@ def tile_two_tower_queue_logits_s9_kernel(
                 in_=s_raw[x][:].rearrange("p g (h q t i) -> p (g h) t q i", q=16, t=4, i=2),
             )
 
-        def sort(x, pair):
+        def sort(x, pair, engine="v"):
             k = source[x].shape[1]
-            ordered[x, pair] = stage.tile([P, 2, k // 2], F32, name="ordered", tag="ordered", bufs=3, align_bytes=64)
+            ordered[x, pair] = stage.tile([P, 2, k // 2], F32, name="ordered", tag="ordered", bufs=4, align_bytes=64)
             flat = raw[x, pair][:].rearrange("p j k -> p (j k)")
             if x == "queue":
                 nc.vector.tensor_copy(
@@ -99,15 +99,33 @@ def tile_two_tower_queue_logits_s9_kernel(
                     in_=flat.rearrange("p (b u e r) -> p b u r e", u=2, e=2, r=8),
                 )
             else:
-                nc.vector.tensor_copy(
-                    out=ordered[x, pair][:].rearrange("p u (c i) -> p c u i", i=4),
-                    in_=flat.bitcast(F32).rearrange("p (c i u) -> p c u i", i=4, u=2),
+                empty(
+                    engine,
+                    ordered[x, pair][:].rearrange("p u (c i) -> p c u i", i=4),
+                    flat.bitcast(F32).rearrange("p (c i u) -> p c u i", i=4, u=2),
                 )
 
-        def turn(x, pair, engines):
+        def turned_tile(x, chunk, g):
+            if (x, chunk, g) not in turned:
+                turned[x, chunk, g] = stage.tile([P, 2 * CH], F32, name="turned", tag="turned", bufs=5, align_bytes=64)
+            return turned[x, chunk, g]
+
+        def empty(engine, out, in_):
+            if engine == "s":
+                nc.scalar.copy(out=out, in_=in_)
+            else:
+                nc.vector.tensor_copy(out=out, in_=in_)
+
+        def turn_chunk(x, chunk, engines):
             for g in range(passes[x]):
+                for half in range(2):
+                    turn(x, 2 * chunk + half, {g: engines[2 * g + half]})
+
+        def turn(x, pair, engines):
+            if isinstance(engines, str):
+                engines = dict(enumerate(engines))
+            for g in engines:
                 bank = new_bank()
-                quarters = bank[:].rearrange("p (j u r) -> p j u r", j=2, u=2)
                 for j in range(2):
                     for u in range(2):
                         first = (j * passes[x] + g) * P
@@ -116,32 +134,49 @@ def tile_two_tower_queue_logits_s9_kernel(
                         else:
                             flat = raw[x, pair][:].rearrange("p j k -> p (j k)").bitcast(F32)
                             block = flat[:, 2 * first + u : 2 * (first + P) : 2]
-                        nc.tensor.transpose(quarters[:, j, u, :], block, ident[:])
-                turned[x, pair, g] = stage.tile([P, CH], F32, name="turned", tag="turned", bufs=8, align_bytes=64)
-                out = turned[x, pair, g][:].rearrange("p (r v) -> p r v", v=4)
-                in_ = bank[:].rearrange("p (v r) -> p r v", v=4)
-                if engines[g] == "s":
-                    nc.scalar.copy(out=out, in_=in_)
-                else:
-                    nc.vector.tensor_copy(out=out, in_=in_)
+                        nc.tensor.transpose(bank[:, (2 * j + u) * P : (2 * j + u + 1) * P], block, ident[:])
+                out = turned_tile(x, pair // 2, g)[:, (pair % 2) * CH : (pair % 2 + 1) * CH]
+                empty(engines[g], out.rearrange("p (r v) -> p r v", v=4), bank[:].rearrange("p (v r) -> p r v", v=4))
 
-        def quantize_rows(x, pair):
-            half = slice((pair % 2) * PAIR, (pair % 2 + 1) * PAIR)
-            for g in range(passes[x]):
-                c, s = mx_tiles((x, pair // 2, g))
-                nc.vector.quantize_mx(
-                    out=c[:, half].bitcast(E4M3), scales=s[:, half], in_=turned[x, pair, g][:].bitcast(BF16)
+        def load_first(g):
+            first_rows[g] = keep.tile([P, 4, KP], BF16, name="first_rows_%d" % g, align_bytes=64)
+            rows = txt[0:CH, g * KP : (g + 1) * KP]
+            nc.sync.dma_start(out=first_rows[g][:], in_=rows.rearrange("(j p) k -> p j k", p=P))
+
+        def turn_first(g, engines):
+            flat = first_rows[g][:].rearrange("p j k -> p (j k)").bitcast(F32)
+            for half in range(2):
+                bank = new_bank()
+                for j in range(2):
+                    for u in range(2):
+                        first = (2 * half + j) * 2 * P
+                        block = flat[:, first + u : first + 2 * P : 2]
+                        nc.tensor.transpose(bank[:, (2 * j + u) * P : (2 * j + u + 1) * P], block, ident[:])
+                out = turned_tile("txt", 0, g)[:, half * CH : (half + 1) * CH]
+                empty(
+                    engines[half],
+                    out.rearrange("p (j r u) -> p j r u", j=2, u=2),
+                    bank[:].rearrange("p (j u r) -> p j r u", j=2, u=2),
                 )
 
-        def tower(x, chunk, h, slots, engines):
+        def quantize_rows(x, chunk, groups, half=None):
+            lo, hi = (0, CH) if half is None else (half * PAIR, (half + 1) * PAIR)
+            for g in groups:
+                c, s = mx_tiles((x, chunk, g))
+                nc.vector.quantize_mx(
+                    out=c[:, lo:hi].bitcast(E4M3), scales=s[:, lo:hi], in_=turned[x, chunk, g][:, 2 * lo : 2 * hi].bitcast(BF16)
+                )
+
+        def tower(x, chunk, h, slots, engines, by_pass=False):
             if (x, chunk, h) not in planar:
                 planar[x, chunk, h] = stage.tile([P, 4, CH], BF16, name="planar", tag="planar", bufs=3, align_bytes=64)
-            for t, engine in zip(slots, engines):
-                bank = new_bank()
-                for g in range(passes[x]):
+            banks = {}
+
+            def one_pass(t, g):
+                if True:
                     col = ((2 * g + h) * 4 + t) * P
                     nc.tensor.matmul_mx(
-                        out=bank[:],
+                        out=banks[t][:],
                         lhsT=w_codes[x, h][:, 2 * (4 * g + t) * P : 2 * (4 * g + t + 1) * P].bitcast(E2M1),
                         lhsT_scale=w_scales[x][:, col : col + P],
                         rhs=codes[x, chunk, g][:].bitcast(E4M3),
@@ -149,6 +184,17 @@ def tile_two_tower_queue_logits_s9_kernel(
                         start=(g == 0),
                         stop=(g == passes[x] - 1),
                     )
+
+            if by_pass:
+                for t in slots:
+                    banks[t] = new_bank()
+                    one_pass(t, 0)
+            for t, engine in zip(slots, engines):
+                if not by_pass:
+                    banks[t] = new_bank()
+                for g in range(1 if by_pass else 0, passes[x]):
+                    one_pass(t, g)
+                bank = banks[t]
                 out = planar[x, chunk, h][:, t, :]
                 bi_col = consts[:, 4 * h + t, 0:1]
                 gain_col = consts[:, 4 * h + t, 1:2]
@@ -203,7 +249,7 @@ def tile_two_tower_queue_logits_s9_kernel(
                     nc.vector.tensor_scalar(out=result, in0=bank[:], scalar1=tau_col, scalar2=None, op0=MULT)
                 out_cols = slice(chunk * CH, (chunk + 1) * CH)
                 if joined == 1:
-                    nc.sync.dma_start(out=dest[m * P : (m + 1) * P, out_cols], in_=result)
+                    (nc.scalar if engine == "s" else nc.sync).dma_start(out=dest[m * P : (m + 1) * P, out_cols], in_=result)
                 elif m % 2 == 1:
                     rows = dest[(m - 1) * P : (m + 1) * P, out_cols]
                     nc.sync.dma_start(out=rows.rearrange("(j p) n -> p j n", j=2), in_=both[:])
@@ -228,8 +274,8 @@ def tile_two_tower_queue_logits_s9_kernel(
             )
             nc.vector.tensor_copy(out=vec_wide[32:40, 0:P], in_=tau_rows[32:40, :])
 
-        def turn_vectors():
-            for h in range(2):
+        def turn_vectors(h):
+            if True:
                 bank = new_bank()
                 for t in range(4):
                     first = (4 * h + t) * P
@@ -248,98 +294,92 @@ def tile_two_tower_queue_logits_s9_kernel(
         clear_scale_rows("img", nc.vector)
 
         load_vectors()
-        load_rows("txt", 0)
-        load_rows("txt", 1)
-        nc.scalar.activation(out=warm[:, 1:2], in_=warm[:, 0:1], func=IDENT, bias=0.0, scale=1.0)
-        load_scale_rows("txt", nc.gpsimd)
-        load_scale_rows("img", nc.gpsimd)
+        load_first(0)
         load_words("txt", 0)
+        load_first(1)
+        nc.scalar.activation(out=warm[:, 1:2], in_=warm[:, 0:1], func=IDENT, bias=0.0, scale=1.0)
+        load_scale_rows("txt", nc.sync)
         load_words("txt", 1)
         load_rows("img", 0)
         load_rows("img", 1)
+        load_scale_rows("img", nc.sync)
         load_words("img", 0)
         load_words("img", 1)
         for x, pair in (("img", 2), ("img", 3), ("queue", 0), ("queue", 1), ("txt", 2), ("txt", 3), ("queue", 2), ("queue", 3)):
             load_rows(x, pair)
         A, B = (0, 1), (2, 3)
         widen_vectors()
-        turn("txt", 0, "ss")
-        quantize_rows("txt", 0)
-        turn("txt", 1, "ss")
+        turn_first(0, "ss")
         order_words("txt", 0)
+        turn_vectors(0)
+        turn_vectors(1)
+        quantize_rows("txt", 0, [0], 0)
+        quantize_rows("txt", 0, [0], 1)
         order_scales("txt")
-        turn_vectors()
-        quantize_rows("txt", 1)
+        turn_first(1, "sv")
+        quantize_rows("txt", 0, [1])
         order_words("txt", 1)
         fold_bias()
         sort("img", 0)
+        tower("txt", 0, 0, range(4), "ssss", by_pass=True)
         sort("img", 1)
-        tower("txt", 0, 0, A, "ss")
-        turn("img", 0, "svs")
-        tower("txt", 0, 0, B, "ss")
-        quantize_rows("img", 0)
-        turn("img", 1, "svs")
+        turn("img", 0, "vvv")
+        tower("txt", 0, 1, [0], "s")
+        turn("img", 1, "sss")
+        quantize_rows("img", 0, range(3), 0)
         order_scales("img")
         order_words("img", 0)
-        tower("txt", 0, 1, range(4), "ssss")
-        quantize_rows("img", 1)
+        tower("txt", 0, 1, [1,2,3], "sss")
+        quantize_rows("img", 0, range(3), 1)
         order_words("img", 1)
         sort("img", 2)
+        sort("img", 3)
         tower("img", 0, 0, range(4), "ssss")
         weave("txt", 0, 0)
-        turn("img", 2, "sss")
-        sort("img", 3)
-        quantize_embedding("txt", 0, 0)
-        weave("txt", 0, 1)
-        tower("img", 0, 1, A, "ss")
-        quantize_rows("img", 2)
-        quantize_embedding("txt", 0, 1)
-        turn("img", 3, "sss")
-        weave("img", 0, 0)
-        tower("img", 0, 1, B, "ss")
-        quantize_rows("img", 3)
-        quantize_embedding("img", 0, 0)
         sort("queue", 0)
+        turn_chunk("img", 1, "ssssss")
+        quantize_embedding("txt", 0, 0)
+        quantize_rows("img", 1, [0])
+        weave("img", 0, 0)
+        quantize_rows("img", 1, [1, 2])
+        tower("img", 0, 1, range(4), "ssss")
+        quantize_embedding("img", 0, 0)
+        sort("queue", 1)
         weave("img", 0, 1)
         tower("img", 1, 0, range(4), "ssss")
-        turn("queue", 0, "ss")
-        quantize_embedding("img", 0, 1)
-        sort("queue", 1)
-        quantize_rows("queue", 0)
-        weave("img", 1, 0)
-        tower("img", 1, 1, A, "ss")
-        logits(A, "emb_txt", 0, "ss")
-        turn("queue", 1, "ss")
         sort("txt", 2)
-        quantize_embedding("img", 1, 0)
-        tower("img", 1, 1, B, "ss")
-        quantize_rows("queue", 1)
-        logits(B, "emb_txt", 0, "sv")
-        turn("txt", 2, "ss")
+        quantize_embedding("img", 0, 1)
+        weave("txt", 0, 1)
+        turn_chunk("queue", 0, "ssss")
         sort("txt", 3)
+        quantize_embedding("txt", 0, 1)
+        tower("img", 1, 1, range(4), "ssss")
+        quantize_rows("queue", 0, A)
+        weave("img", 1, 0)
+        turn_chunk("txt", 1, "ssvs")
+        quantize_embedding("img", 1, 0)
         weave("img", 1, 1)
-        logits(A, "queue", 0, "ss")
-        quantize_rows("txt", 2)
-        turn("txt", 3, "ss")
+        logits(range(4), "emb_txt", 0, "ssss")
+        quantize_rows("txt", 1, A)
+        logits(range(4), "queue", 0, "ssss")
         quantize_embedding("img", 1, 1)
-        logits(B, "queue", 0, "ss")
-        quantize_rows("txt", 3)
         sort("queue", 2)
-        logits((4, 5), "emb_txt", 0, "sv")
-        tower("txt", 1, 0, range(4), "svss")
-        turn("queue", 2, "ss")
         sort("queue", 3)
+        tower("txt", 1, 0, A, "ss")
+        logits((4, 5), "emb_txt", 0, "ss")
+        tower("txt", 1, 0, B, "sv")
+        turn_chunk("queue", 1, "svsv")
+        logits((6, 7), "emb_txt", 0, "ss")
+        quantize_rows("queue", 1, A)
         weave("txt", 1, 0)
         tower("txt", 1, 1, A, "ss")
-        quantize_rows("queue", 2)
-        logits((6, 7), "emb_txt", 0, "ss")
+        logits(range(4, 8), "queue", 0, "ssvs")
         quantize_embedding("txt", 1, 0)
+        logits(A, "queue", 1, "sv")
         tower("txt", 1, 1, B, "sv")
-        turn("queue", 3, "ss")
         weave("txt", 1, 1)
-        logits(range(4, 8), "queue", 0, "ssss")
-        quantize_rows("queue", 3)
+        logits(B, "queue", 1, "ss")
         quantize_embedding("txt", 1, 1)
-        logits(range(0, 8), "queue", 1, "svsvsvsv")
-        logits(range(0, 6), "emb_txt", 1, "svsvsv")
-        logits((6, 7), "emb_txt", 1, "sv", joined=1)
+        logits(range(4, 8), "queue", 1, "ssvs")
+        logits(range(0, 6), "emb_txt", 1, "vsvsvs")
+        logits(range(6, 8), "emb_txt", 1, "vs", joined=1)

from contextlib import ExitStack

import concourse.mybir as mybir
from concourse.masks import make_identity

M, N, Q, KI, KT, D = 1024, 1024, 1024, 1536, 1024, 1024
FLOPS = 2 * M * KI * D + 2 * N * KT * D + 2 * M * D * (N + Q)

F32 = mybir.dt.float32
BF16 = mybir.dt.bfloat16
I32 = mybir.dt.int32
U32 = mybir.dt.uint32
U8 = mybir.dt.uint8
E4M3 = mybir.dt.float8_e4m3fn_x4
E5M2 = mybir.dt.float8_e5m2_x4
E2M1 = mybir.dt.float4_e2m1fn_x4
IDENT = mybir.ActivationFunctionType.Identity
ADD = mybir.AluOpType.add
MULT = mybir.AluOpType.mult

P = 128
KP = 512
CH = 512
PAIR = 256


def tile_two_tower_queue_logits_s9_kernel(
    tc, img, wi_words, wi_scales, bi, gain, txt, wt_words, wt_scales, bt, queue, tau, out_0, out_1
):
    nc = tc.nc
    with ExitStack() as ctx:
        keep = ctx.enter_context(tc.tile_pool(name="keep", bufs=1))
        stage = ctx.enter_context(tc.tile_pool(name="stage", bufs=1))
        psum = ctx.enter_context(tc.psum_pool(name="psum", bufs=8))
        ctx.enter_context(tc.manual_schedule())

        source = {"img": img, "txt": txt, "queue": queue}
        passes = {"img": KI // KP, "txt": KT // KP, "queue": D // KP}
        words_in = {"img": wi_words, "txt": wt_words}
        scales_in = {"img": wi_scales, "txt": wt_scales}
        raw, ordered, turned, first_rows = {}, {}, {}, {}
        w_raw, s_raw, w_codes, w_scales = {}, {}, {}, {}
        codes, scales, planar, woven, results = {}, {}, {}, {}, {}

        def new_bank():
            return psum.tile([P, CH], F32, name="bank", tag="bank")

        def mx_tiles(key):
            if key not in codes:
                label = "_".join(str(k) for k in key)
                codes[key] = keep.tile([P, CH], U32, name="codes_" + label, align_bytes=64)
                scales[key] = keep.tile([P, CH], U8, name="scales_" + label, align_bytes=64)
            return codes[key], scales[key]

        def load_rows(x, pair):
            k = source[x].shape[1]
            raw[x, pair] = keep.tile([P, 2, k], BF16, name="raw_%s_%d" % (x, pair), align_bytes=64)
            rows = source[x][pair * PAIR : (pair + 1) * PAIR, :]
            nc.sync.dma_start(out=raw[x, pair][:], in_=rows.rearrange("(p j) k -> p j k", j=2))

        def clear_scale_rows(x, engine):
            s_raw[x] = keep.tile([P, passes[x], D // 4], I32, name="s_raw_" + x, align_bytes=64)
            engine.memset(s_raw[x][:], 0)

        def load_words(x, h):
            w_raw[x, h] = keep.tile([P, passes[x], KP // 2], I32, name="w_raw_%s_%d" % (x, h), align_bytes=64)
            half = words_in[x].bitcast(I32)[:, :, h * KP // 2 : (h + 1) * KP // 2]
            nc.sync.dma_start(out=w_raw[x, h][:], in_=half.rearrange("g p n -> p g n"))

        def load_scale_rows(x, engine):
            rows = scales_in[x].bitcast(I32)
            for quad in range(4):
                engine.dma_start(
                    out=s_raw[x][32 * quad : 32 * quad + 4, :, :],
                    in_=rows[:, 4 * quad : 4 * quad + 4, :].rearrange("g r n -> r g n"),
                )

        def order_words(x, h):
            w_codes[x, h] = keep.tile([P, passes[x] * 2 * KP], U8, name="w_codes_%s_%d" % (x, h), align_bytes=256)
            nc.vector.tensor_copy(
                out=w_codes[x, h][:].bitcast(I32).rearrange("p (g t q i) -> p g q t i", t=4, q=16, i=4),
                in_=w_raw[x, h][:].rearrange("p g (q t i) -> p g q t i", t=4, i=4),
            )

        def order_scales(x):
            w_scales[x] = keep.tile([P, passes[x] * D], U8, name="w_scales_" + x, align_bytes=256)
            nc.vector.tensor_copy(
                out=w_scales[x][:].bitcast(I32).rearrange("p (h t q i) -> p h t q i", t=4, q=16, i=2),
                in_=s_raw[x][:].rearrange("p g (h q t i) -> p (g h) t q i", q=16, t=4, i=2),
            )

        def sort(x, pair, engine="v"):
            k = source[x].shape[1]
            ordered[x, pair] = stage.tile([P, 2, k // 2], F32, name="ordered", tag="ordered", bufs=4, align_bytes=64)
            flat = raw[x, pair][:].rearrange("p j k -> p (j k)")
            if x == "queue":
                nc.vector.tensor_copy(
                    out=ordered[x, pair][:].bitcast(BF16).rearrange("p u (b r e) -> p b u r e", r=8, e=2),
                    in_=flat.rearrange("p (b u e r) -> p b u r e", u=2, e=2, r=8),
                )
            else:
                empty(
                    engine,
                    ordered[x, pair][:].rearrange("p u (c i) -> p c u i", i=4),
                    flat.bitcast(F32).rearrange("p (c i u) -> p c u i", i=4, u=2),
                )

        def turned_tile(x, chunk, g):
            if (x, chunk, g) not in turned:
                turned[x, chunk, g] = stage.tile([P, 2 * CH], F32, name="turned", tag="turned", bufs=5, align_bytes=64)
            return turned[x, chunk, g]

        def empty(engine, out, in_):
            if engine == "s":
                nc.scalar.copy(out=out, in_=in_)
            else:
                nc.vector.tensor_copy(out=out, in_=in_)

        def turn_chunk(x, chunk, engines):
            for g in range(passes[x]):
                for half in range(2):
                    turn(x, 2 * chunk + half, {g: engines[2 * g + half]})

        def turn(x, pair, engines):
            if isinstance(engines, str):
                engines = dict(enumerate(engines))
            for g in engines:
                bank = new_bank()
                for j in range(2):
                    for u in range(2):
                        first = (j * passes[x] + g) * P
                        if (x, pair) in ordered:
                            block = ordered[x, pair][:, u, first : first + P]
                        else:
                            flat = raw[x, pair][:].rearrange("p j k -> p (j k)").bitcast(F32)
                            block = flat[:, 2 * first + u : 2 * (first + P) : 2]
                        nc.tensor.transpose(bank[:, (2 * j + u) * P : (2 * j + u + 1) * P], block, ident[:])
                out = turned_tile(x, pair // 2, g)[:, (pair % 2) * CH : (pair % 2 + 1) * CH]
                empty(engines[g], out.rearrange("p (r v) -> p r v", v=4), bank[:].rearrange("p (v r) -> p r v", v=4))

        def load_first(g):
            first_rows[g] = keep.tile([P, 4, KP], BF16, name="first_rows_%d" % g, align_bytes=64)
            rows = txt[0:CH, g * KP : (g + 1) * KP]
            nc.sync.dma_start(out=first_rows[g][:], in_=rows.rearrange("(j p) k -> p j k", p=P))

        def turn_first(g, engines):
            flat = first_rows[g][:].rearrange("p j k -> p (j k)").bitcast(F32)
            for half in range(2):
                bank = new_bank()
                for j in range(2):
                    for u in range(2):
                        first = (2 * half + j) * 2 * P
                        block = flat[:, first + u : first + 2 * P : 2]
                        nc.tensor.transpose(bank[:, (2 * j + u) * P : (2 * j + u + 1) * P], block, ident[:])
                out = turned_tile("txt", 0, g)[:, half * CH : (half + 1) * CH]
                empty(
                    engines[half],
                    out.rearrange("p (j r u) -> p j r u", j=2, u=2),
                    bank[:].rearrange("p (j u r) -> p j r u", j=2, u=2),
                )

        def quantize_rows(x, chunk, groups, half=None):
            lo, hi = (0, CH) if half is None else (half * PAIR, (half + 1) * PAIR)
            for g in groups:
                c, s = mx_tiles((x, chunk, g))
                nc.vector.quantize_mx(
                    out=c[:, lo:hi].bitcast(E4M3), scales=s[:, lo:hi], in_=turned[x, chunk, g][:, 2 * lo : 2 * hi].bitcast(BF16)
                )

        def tower(x, chunk, h, slots, engines, by_pass=False):
            if (x, chunk, h) not in planar:
                planar[x, chunk, h] = stage.tile([P, 4, CH], BF16, name="planar", tag="planar", bufs=3, align_bytes=64)
            banks = {}

            def one_pass(t, g):
                if True:
                    col = ((2 * g + h) * 4 + t) * P
                    nc.tensor.matmul_mx(
                        out=banks[t][:],
                        lhsT=w_codes[x, h][:, 2 * (4 * g + t) * P : 2 * (4 * g + t + 1) * P].bitcast(E2M1),
                        lhsT_scale=w_scales[x][:, col : col + P],
                        rhs=codes[x, chunk, g][:].bitcast(E4M3),
                        rhs_scale=scales[x, chunk, g][:],
                        start=(g == 0),
                        stop=(g == passes[x] - 1),
                    )

            if by_pass:
                for t in slots:
                    banks[t] = new_bank()
                    one_pass(t, 0)
            for t, engine in zip(slots, engines):
                if not by_pass:
                    banks[t] = new_bank()
                for g in range(1 if by_pass else 0, passes[x]):
                    one_pass(t, g)
                bank = banks[t]
                out = planar[x, chunk, h][:, t, :]
                bi_col = consts[:, 4 * h + t, 0:1]
                gain_col = consts[:, 4 * h + t, 1:2]
                bt_col = consts[:, 4 * h + t, 2:3]
                if x == "img" and engine == "s":
                    nc.scalar.activation(out=out, in_=bank[:], func=IDENT, bias=bi_gain[:, 4 * h + t, :], scale=gain_col)
                elif x == "img":
                    nc.vector.tensor_scalar(out=out, in0=bank[:], scalar1=bi_col, scalar2=gain_col, op0=ADD, op1=MULT)
                elif engine == "s":
                    nc.scalar.activation(out=out, in_=bank[:], func=IDENT, bias=bt_col, scale=1.0)
                else:
                    nc.vector.tensor_scalar(out=out, in0=bank[:], scalar1=bt_col, scalar2=None, op0=ADD)

        def weave(x, chunk, h):
            woven[x, chunk, h] = stage.tile([P, CH, 4], BF16, name="woven", tag="woven", bufs=2, align_bytes=64)
            nc.vector.tensor_copy(
                out=woven[x, chunk, h][:].rearrange("p (c i) t -> p c t i", i=4),
                in_=planar[x, chunk, h][:].rearrange("p t (c i) -> p c t i", i=4),
            )

        def quantize_embedding(x, chunk, h):
            c, s = mx_tiles(("emb_" + x, chunk, h))
            nc.vector.quantize_mx(
                out=c[:].bitcast(E5M2 if x == "img" else E4M3),
                scales=s[:],
                in_=woven[x, chunk, h][:].rearrange("p c t -> p (c t)"),
            )

        def logits(tiles, partner, chunk, engines, joined=2):
            dest = out_1 if partner == "queue" else out_0
            for m, engine in zip(tiles, engines):
                bank = new_bank()
                cols = slice((m % 4) * P, (m % 4 + 1) * P)
                for h in range(2):
                    nc.tensor.matmul_mx(
                        out=bank[:],
                        lhsT=codes["emb_img", m // 4, h][:, cols].bitcast(E5M2),
                        lhsT_scale=scales["emb_img", m // 4, h][:, cols],
                        rhs=codes[partner, chunk, h][:].bitcast(E4M3),
                        rhs_scale=scales[partner, chunk, h][:],
                        start=(h == 0),
                        stop=(h == 1),
                    )
                if m % 2 == 0:
                    results[partner, chunk, m // 2] = stage.tile([P, 2, CH], F32, name="result", tag="result", bufs=5, align_bytes=64)
                both = results[partner, chunk, m // 2]
                result = both[:, m % 2, :]
                tau_col = consts[:, 0, 32 + m : 33 + m]
                if engine == "s":
                    nc.scalar.activation(out=result, in_=bank[:], func=IDENT, bias=0.0, scale=tau_col)
                else:
                    nc.vector.tensor_scalar(out=result, in0=bank[:], scalar1=tau_col, scalar2=None, op0=MULT)
                out_cols = slice(chunk * CH, (chunk + 1) * CH)
                if joined == 1:
                    (nc.scalar if engine == "s" else nc.sync).dma_start(out=dest[m * P : (m + 1) * P, out_cols], in_=result)
                elif m % 2 == 1:
                    rows = dest[(m - 1) * P : (m + 1) * P, out_cols]
                    nc.sync.dma_start(out=rows.rearrange("(j p) n -> p j n", j=2), in_=both[:])

        ident = keep.tile([P, P], F32, name="ident", align_bytes=64)
        vec_rows = keep.tile([3, D], BF16, name="vec_rows", align_bytes=64)
        tau_rows = keep.tile([40, P], BF16, name="tau_rows", align_bytes=64)
        vec_wide = keep.tile([P, D], F32, name="vec_wide", align_bytes=64)
        consts = keep.tile([P, 8, 40], F32, name="consts", align_bytes=64)
        bi_gain = keep.tile([P, 8, 1], F32, name="bi_gain", align_bytes=64)
        warm = keep.tile([P, 2], F32, name="warm", align_bytes=64)

        def load_vectors():
            for v, vec in enumerate((bi, gain, bt)):
                nc.scalar.dma_start(out=vec_rows[v : v + 1, :], in_=vec.rearrange("(a d) -> a d", a=1))
            nc.scalar.dma_start(out=tau_rows[32:40, :], in_=tau.rearrange("(m p) -> m p", p=P))

        def widen_vectors():
            nc.vector.tensor_copy(
                out=vec_wide[0:3, :].rearrange("v (h t q r) -> v h q t r", h=2, t=4, r=8),
                in_=vec_rows[:].rearrange("v (h q t r) -> v h q t r", h=2, t=4, r=8),
            )
            nc.vector.tensor_copy(out=vec_wide[32:40, 0:P], in_=tau_rows[32:40, :])

        def turn_vectors(h):
            if True:
                bank = new_bank()
                for t in range(4):
                    first = (4 * h + t) * P
                    nc.tensor.transpose(bank[:, t * P : (t + 1) * P], vec_wide[:, first : first + P], ident[:])
                nc.scalar.copy(
                    out=consts[:, 4 * h : 4 * h + 4, :], in_=bank[:].rearrange("p (t c) -> p t c", t=4)[:, :, 0:40]
                )

        def fold_bias():
            nc.vector.tensor_tensor(out=bi_gain[:], in0=consts[:, :, 0:1], in1=consts[:, :, 1:2], op=MULT)

        make_identity(nc, ident[:])
        clear_scale_rows("txt", nc.vector)
        nc.vector.memset(warm[:, 0:1], 0.0)
        nc.vector.memset(vec_wide[:], 0.0)
        clear_scale_rows("img", nc.vector)

        load_vectors()
        load_first(0)
        load_words("txt", 0)
        load_first(1)
        nc.scalar.activation(out=warm[:, 1:2], in_=warm[:, 0:1], func=IDENT, bias=0.0, scale=1.0)
        load_scale_rows("txt", nc.sync)
        load_words("txt", 1)
        load_rows("img", 0)
        load_rows("img", 1)
        load_scale_rows("img", nc.sync)
        load_words("img", 0)
        load_words("img", 1)
        for x, pair in (("img", 2), ("img", 3), ("queue", 0), ("queue", 1), ("txt", 2), ("txt", 3), ("queue", 2), ("queue", 3)):
            load_rows(x, pair)
        A, B = (0, 1), (2, 3)
        widen_vectors()
        turn_first(0, "ss")
        order_words("txt", 0)
        turn_vectors(0)
        turn_vectors(1)
        quantize_rows("txt", 0, [0], 0)
        quantize_rows("txt", 0, [0], 1)
        order_scales("txt")
        turn_first(1, "sv")
        quantize_rows("txt", 0, [1])
        order_words("txt", 1)
        fold_bias()
        sort("img", 0)
        tower("txt", 0, 0, range(4), "ssss", by_pass=True)
        sort("img", 1)
        turn("img", 0, "vvv")
        tower("txt", 0, 1, [0], "s")
        turn("img", 1, "sss")
        quantize_rows("img", 0, range(3), 0)
        order_scales("img")
        order_words("img", 0)
        tower("txt", 0, 1, [1,2,3], "sss")
        quantize_rows("img", 0, range(3), 1)
        order_words("img", 1)
        sort("img", 2)
        sort("img", 3)
        tower("img", 0, 0, range(4), "ssss")
        weave("txt", 0, 0)
        sort("queue", 0)
        turn_chunk("img", 1, "ssssss")
        quantize_embedding("txt", 0, 0)
        quantize_rows("img", 1, [0])
        weave("img", 0, 0)
        quantize_rows("img", 1, [1, 2])
        tower("img", 0, 1, range(4), "ssss")
        quantize_embedding("img", 0, 0)
        sort("queue", 1)
        weave("img", 0, 1)
        tower("img", 1, 0, range(4), "ssss")
        sort("txt", 2)
        quantize_embedding("img", 0, 1)
        weave("txt", 0, 1)
        turn_chunk("queue", 0, "ssss")
        sort("txt", 3)
        quantize_embedding("txt", 0, 1)
        tower("img", 1, 1, range(4), "ssss")
        quantize_rows("queue", 0, A)
        weave("img", 1, 0)
        turn_chunk("txt", 1, "ssvs")
        quantize_embedding("img", 1, 0)
        weave("img", 1, 1)
        logits(range(4), "emb_txt", 0, "ssss")
        quantize_rows("txt", 1, A)
        logits(range(4), "queue", 0, "ssss")
        quantize_embedding("img", 1, 1)
        sort("queue", 2)
        sort("queue", 3)
        tower("txt", 1, 0, A, "ss")
        logits((4, 5), "emb_txt", 0, "ss")
        tower("txt", 1, 0, B, "sv")
        turn_chunk("queue", 1, "svsv")
        logits((6, 7), "emb_txt", 0, "ss")
        quantize_rows("queue", 1, A)
        weave("txt", 1, 0)
        tower("txt", 1, 1, A, "ss")
        logits(range(4, 8), "queue", 0, "ssvs")
        quantize_embedding("txt", 1, 0)
        logits(A, "queue", 1, "sv")
        tower("txt", 1, 1, B, "sv")
        weave("txt", 1, 1)
        logits(B, "queue", 1, "ss")
        quantize_embedding("txt", 1, 1)
        logits(range(4, 8), "queue", 1, "ssvs")
        logits(range(0, 6), "emb_txt", 1, "vsvsvs")
        logits(range(6, 8), "emb_txt", 1, "vs", joined=1)
